import numpy as np
import ml_dtypes


def mxq(x, axis, fmt="e4m3"):
    dtype, down = {"e4m3": (ml_dtypes.float8_e4m3fn, 7), "e5m2": (ml_dtypes.float8_e5m2, 14)}[fmt]
    v = np.moveaxis(np.asarray(x, np.float32).astype(ml_dtypes.bfloat16).astype(np.float64), axis, -1)
    blocks = v.reshape(v.shape[:-1] + (-1, 32))
    amax = np.abs(blocks).max(-1, keepdims=True)
    byte = np.maximum(np.where(amax > 0, np.frexp(amax)[1] - 1 + 127, 0) - down, 1)
    scale = np.exp2(byte - 127.0)
    codes = (blocks / scale).astype(np.float32).astype(dtype).astype(np.float64)
    return np.moveaxis((codes * scale).reshape(v.shape), -1, axis)


WIDE = False


def mx_kscale(k):
    if not WIDE:
        return np.ones(k)
    levels = np.array([10, -10, 5, -5, 0])
    if k % 512:
        return np.exp2(np.random.permutation(np.resize(levels, k // 32))).repeat(32)
    a = np.empty((k // 512, 16))
    for p in range(k // 512):
        a[p, :8] = np.random.permutation(np.resize(levels, 8))
        for g in range(8):
            far = levels[np.abs(levels - a[p, g]) >= 10]
            a[p, g + 8] = far[np.random.randint(len(far))]
    return np.exp2(a.ravel()).repeat(32)


def f64(x):
    return np.asarray(x).astype(np.float64)


def striped(idx):
    return np.tile(np.asarray(idx).reshape(-1, 16).T, (8, 1)).astype(np.uint16)


def unstriped(offs):
    return offs[:16].T.reshape(-1).astype(np.int64)


E2M1 = np.array([0.0, 0.5, 1.0, 1.5, 2.0, 3.0, 4.0, 6.0, -0.0, -0.5, -1.0, -1.5, -2.0, -3.0, -4.0, -6.0])


def pack_weight(w, fmt):
    k, n = w.shape
    w = f64(np.asarray(w, np.float32).astype(ml_dtypes.bfloat16)).reshape(k // 32, 32, n)
    amax = np.abs(w).max(1)
    if fmt == "e4m3":
        byte = np.frexp(amax)[1] - 1 + 127 - 7
    else:
        mant, ex = np.frexp(amax / 6.0)
        byte = np.where(mant > 0.5, ex, ex - 1) + 127
    byte = np.clip(np.where(amax > 0, byte, 1), 1, 254)
    scaled = (w * np.exp2(127.0 - byte)[:, None, :]).reshape(k, n).astype(np.float32)
    by_word = np.ascontiguousarray(scaled.reshape(k // 512, 128, 4, n).transpose(0, 1, 3, 2))
    if fmt == "e4m3":
        words = by_word.astype(ml_dtypes.float8_e4m3fn).view(np.uint8)
    else:
        c = by_word.astype(ml_dtypes.float4_e2m1fn).view(np.uint8) & 0xF
        words = (c[..., 0::2] | (c[..., 1::2] << 4)).reshape(k // 512, 128, 2 * n)
    return np.ascontiguousarray(words), np.ascontiguousarray(byte.astype(np.uint8).reshape(k // 512, 16, n))


def unpack_weight(words, scales, fmt):
    g, _, n = scales.shape
    words = np.ascontiguousarray(words).reshape(g, 128, n, -1)
    if fmt == "e4m3":
        vals = words.view(ml_dtypes.float8_e4m3fn).astype(np.float64)
    else:
        nib = np.empty((g, 128, n, 4), np.uint8)
        nib[..., 0::2] = words & 0xF
        nib[..., 1::2] = words >> 4
        vals = E2M1[nib]
    vals = vals * np.repeat(np.exp2(scales.astype(np.float64) - 127.0), 8, axis=1)[..., None]
    return vals.transpose(0, 1, 3, 2).reshape(g * 512, n)


K, T, J, I, N, R, S = 512, 1024, 512, 512, 512, 512, 512


def setup_inputs():
    n = np.random.standard_normal
    idx = np.random.permutation(T)[:J]
    idx2 = np.random.permutation(T)[:I]
    fk = mx_kscale(K)
    fr = mx_kscale(R)
    fs = mx_kscale(S)
    xqp = pack_weight(n((K, T)) / fk[:, None], "e4m3")
    wsp = pack_weight(n((K, N)) * 1 / np.sqrt(K) * fk[:, None], "e2m1")
    lap = pack_weight(n((K, R)) * 1 / np.sqrt(K) * fk[:, None] * fr, "e4m3")
    uap = pack_weight(n((R, N)) * 1 / np.sqrt(R) / fr[:, None], "e2m1")
    lbp = pack_weight(n((K, S)) * 1 / np.sqrt(K) * fk[:, None] * fs, "e4m3")
    ubp = pack_weight(n((S, N)) * 1 / np.sqrt(S) / fs[:, None], "e2m1")
    return {
        "xq_words": xqp[0],
        "xq_scales": xqp[1],
        "ws_words": wsp[0],
        "ws_scales": wsp[1],
        "la_words": lap[0],
        "la_scales": lap[1],
        "ua_words": uap[0],
        "ua_scales": uap[1],
        "lb_words": lbp[0],
        "lb_scales": lbp[1],
        "ub_words": ubp[0],
        "ub_scales": ubp[1],
        "offs": striped(idx),
        "offs2": striped(idx2),
    }


def reference(xq_words, xq_scales, ws_words, ws_scales, la_words, la_scales, ua_words, ua_scales, lb_words, lb_scales, ub_words, ub_scales, offs, offs2):
    idx = unstriped(offs)
    idx2 = unstriped(offs2)
    xqu = unpack_weight(xq_words, xq_scales, "e4m3")
    wsu = unpack_weight(ws_words, ws_scales, "e2m1")
    lau = unpack_weight(la_words, la_scales, "e4m3")
    uau = unpack_weight(ua_words, ua_scales, "e2m1")
    lbu = unpack_weight(lb_words, lb_scales, "e4m3")
    ubu = unpack_weight(ub_words, ub_scales, "e2m1")
    b = wsu.T @ xqu
    xqidxg = xqu[:, idx]
    u = lau.T @ xqidxg
    xqidx2g = xqu[:, idx2]
    v = lbu.T @ xqidx2g
    uq = mxq(u, 0, "e4m3")
    p = uau.T @ uq
    vq = mxq(v, 0, "e4m3")
    q = ubu.T @ vq
    pg = np.zeros((N, T))
    pg[:, idx] = p
    qg = np.zeros((N, T))
    qg[:, idx2] = q
    y = 0.4 * b + pg + qg
    return y

@@ -1,0 +1,295 @@
+from contextlib import ExitStack
+
+import concourse.mybir as mybir
+from concourse.masks import make_identity
+
+K, T, J, N, R = 512, 1024, 512, 512, 512
+FLOPS = 2 * K * N * T + 2 * (2 * K * R * J + 2 * R * N * J)
+
+F32 = mybir.dt.float32
+BF16 = mybir.dt.bfloat16
+I32 = mybir.dt.int32
+U32 = mybir.dt.uint32
+U16 = mybir.dt.uint16
+U8 = mybir.dt.uint8
+FP8X4 = mybir.dt.float8_e4m3fn_x4
+FP4X4 = mybir.dt.float4_e2m1fn_x4
+COPY = mybir.ActivationFunctionType.Copy
+ADD = mybir.AluOpType.add
+
+P = 128
+PACK = 4
+BANK = 512
+BASE_GAIN = 0.4
+
+
+def tile_list_two_experts_on_base_kernel(
+    tc, xq_words, xq_scales, ws_words, ws_scales, la_words, la_scales, ua_words, ua_scales,
+    lb_words, lb_scales, ub_words, ub_scales, offs, offs2, out,
+):
+    nc = tc.nc
+    with ExitStack() as ctx:
+        keep = ctx.enter_context(tc.tile_pool(name="keep", bufs=1))
+        shared = ctx.enter_context(tc.tile_pool(name="shared", bufs=1))
+        psum = ctx.enter_context(tc.psum_pool(name="psum", bufs=1))
+
+        def sb(name, shape, dtype, tag=None):
+            return keep.tile(shape, dtype, name=name, tag=tag or name, align_bytes=64)
+
+        def bank(b, name):
+            return psum.tile([P, BANK], F32, name=name, tag="bank%d" % b)
+
+        def load_scale_rows(plane, rows, first):
+            for q in range(4):
+                nc.sync.dma_start(
+                    out=plane[32 * q + first : 32 * q + first + 4, :].bitcast(I32),
+                    in_=rows[0, 4 * q : 4 * q + 4, :].bitcast(I32),
+                )
+
+        def fp8_words(words):
+            return words[0].rearrange("p n t -> p (n t)").bitcast(I32)
+
+        list_a = keep.tile([P, J // 16], U16, name="list_a")
+        list_b = keep.tile([P, J // 16], U16, name="list_b")
+        x_words = sb("x_words", [P, T], I32)
+        x_plane = sb("x_plane", [P, T], U8)
+        low_plane_raw = shared.tile([P, R], U8, name="low_plane_raw", align_bytes=64, offset=4 * J - 256)
+        ua_plane = sb("ua_plane", [P, N], U8)
+        late_planes = sb("late_planes", [P, 2 * N], U8)
+        la_raw = sb("la_raw", [P, R], I32, tag="raw_words")
+        ua_w = sb("ua_w", [P, 2 * N], U8)
+        pages = [[sb("page%d%d" % (e, s), [P, T], F32) for s in range(2)] for e in range(2)]
+        ident = sb("ident", [P, P], F32)
+
+        nc.gpsimd.memset(x_plane[:].bitcast(I32), 0)
+        nc.gpsimd.memset(low_plane_raw[:].bitcast(I32), 0)
+        nc.vector.memset(ua_plane[:].bitcast(I32), 0)
+        nc.sync.dma_start(list_a[:], offs)
+        nc.sync.dma_start(list_b[:], offs2)
+        load_scale_rows(x_plane, xq_scales, 0)
+        nc.sync.dma_start(out=x_words[:], in_=fp8_words(xq_words))
+        nc.sync.dma_start(out=la_raw[:], in_=fp8_words(la_words))
+        load_scale_rows(low_plane_raw, la_scales, 0)
+        load_scale_rows(low_plane_raw, lb_scales, 4)
+        nc.sync.dma_start(out=ua_w[:].bitcast(I32), in_=ua_words[0].bitcast(I32))
+        load_scale_rows(ua_plane, ua_scales, 0)
+        for e in range(2):
+            for s in range(2):
+                nc.vector.memset(pages[e][s][:], 0.0)
+        nc.vector.memset(late_planes[:].bitcast(I32), 0)
+        make_identity(nc, ident[:])
+
+        lists = [list_a, list_b]
+        g_words = [sb("g_words0", [P, J], I32, tag="first_words")]
+        g_plane = [sb("g_plane0", [P, J], U8)]
+        low_words = [sb("low_words%d" % e, [P, R], I32) for e in range(2)]
+        low_plane = sb("low_plane", [P, R], U8)
+        mid_bf = [[sb("mid_bf%d%d" % (e, h), [P, 2, P, PACK], BF16) for h in range(2)] for e in range(2)]
+        mid_words = [sb("mid_words%d" % e, [P, J], I32) for e in range(2)]
+        mid_plane = [sb("mid_plane%d" % e, [P, J], U8) for e in range(2)]
+        up_words = [ua_w]
+        up_planes = [ua_plane[:], late_planes[:, 0:N]]
+        ws_plane = late_planes[:, N : 2 * N]
+        results = [[sb("res%d%d" % (e, nt), [P, J], F32) for nt in range(4)] for e in range(2)]
+
+        def gather_plane(e):
+            nc.vector.tensor_copy(out=g_plane[e][:], in_=x_plane[:].indirect(lists[e][:]))
+
+        def gather_words(e, lo, hi):
+            nc.vector.tensor_copy(
+                out=g_words[e][:, lo:hi].bitcast(U32),
+                in_=x_words[:].bitcast(U32).indirect(lists[e][:, lo // 16 : hi // 16]),
+            )
+
+        def deal(dst, src):
+            nc.vector.tensor_copy(
+                out=dst.rearrange("p (t m) -> p m t", t=PACK), in_=src.rearrange("p (m t) -> p m t", t=PACK)
+            )
+
+        def lower(e, c, b):
+            acc = bank(b, "low%d%d" % (e, c))
+            cols = slice(P * c, P * (c + 1))
+            for t in range(PACK):
+                tc_ = slice(P * t, P * (t + 1))
+                nc.tensor.matmul_mx(
+                    out=acc[:, tc_],
+                    lhsT=low_words[e][:, tc_].bitcast(FP8X4),
+                    lhsT_scale=low_plane[4 * e : P, tc_],
+                    rhs=g_words[e][:, cols].bitcast(FP8X4),
+                    rhs_scale=g_plane[e][:, cols],
+                    start=True,
+                    stop=True,
+                )
+            nc.scalar.copy(out=mid_bf[e][c // 2][:, c % 2, :, :], in_=acc[:].rearrange("p (t j) -> p j t", t=PACK))
+
+        def quantise(e, h):
+            cols = slice(256 * h, 256 * (h + 1))
+            nc.vector.quantize_mx(
+                out=mid_words[e][:, cols].bitcast(FP8X4),
+                scales=mid_plane[e][:, cols],
+                in_=mid_bf[e][h][:].rearrange("p c j t -> p (c j t)"),
+            )
+
+        def upper(e, nt, b, lo, hi):
+            acc = bank(b, "up%d%d_%d" % (e, nt, lo))
+            nc.tensor.matmul_mx(
+                out=acc[:, 0 : hi - lo],
+                lhsT=up_words[e][:, 2 * P * nt : 2 * P * (nt + 1)].bitcast(FP4X4),
+                lhsT_scale=up_planes[e][:, P * nt : P * (nt + 1)],
+                rhs=mid_words[e][:, lo:hi].bitcast(FP8X4),
+                rhs_scale=mid_plane[e][:, lo:hi],
+                start=True,
+                stop=True,
+            )
+            nc.scalar.copy(out=results[e][nt][:, lo:hi], in_=acc[:, 0 : hi - lo])
+
+        def scatter(e, nt, lo, hi):
+            nc.vector.tensor_copy(
+                out=pages[e][nt % 2][:].indirect(lists[e][:, lo // 16 : hi // 16]),
+                in_=results[e][nt][:, lo:hi],
+            )
+
+        def turn_add(acc, c, src, start, stop):
+            nc.tensor.matmul(
+                out=acc[:, P * c : P * (c + 1)], lhsT=src, rhs=ident[:], start=start, stop=stop, is_transpose=True
+            )
+
+        based = {}
+        turned = {}
+        summed = {}
+
+        def base(nt):
+            based[nt] = sb("based%d" % nt, [P, T], F32)
+            for h in range(2):
+                acc = bank(4 + h, "base%d%d" % (nt, h))
+                cols = slice(BANK * h, BANK * (h + 1))
+                if nt < 3:
+                    nc.tensor.matmul_mx(
+                        out=acc[:],
+                        lhsT=ws_w[:, 2 * P * nt : 2 * P * (nt + 1)].bitcast(FP4X4),
+                        lhsT_scale=ws_plane[:, P * nt : P * (nt + 1)],
+                        rhs=x_words[:, cols].bitcast(FP8X4),
+                        rhs_scale=x_plane[:, cols],
+                        start=True,
+                        stop=True,
+                    )
+                else:
+                    for c in range(4):
+                        toks = slice(BANK * h + P * c, BANK * h + P * (c + 1))
+                        nc.tensor.matmul_mx(
+                            out=acc[:, P * c : P * (c + 1)],
+                            lhsT=x_words[:, toks].bitcast(FP8X4),
+                            lhsT_scale=x_plane[:, toks],
+                            rhs=ws_w[:, 2 * P * nt : 2 * P * (nt + 1)].bitcast(FP4X4),
+                            rhs_scale=ws_plane[:, P * nt : P * (nt + 1)],
+                            start=True,
+                            stop=True,
+                        )
+                nc.scalar.activation(out=based[nt][:, cols], in_=acc[:], func=COPY, scale=BASE_GAIN)
+
+        def turn_half(acc, src, h, start, stop):
+            for c in range(4):
+                tb = 4 * h + c
+                turn_add(acc, c, src[:, P * tb : P * (tb + 1)], start and c == 0, stop and c == 3)
+
+        def turn_base(nt):
+            for h in range(2):
+                if nt < 3:
+                    turned[nt, h] = bank((2, 6, 2)[nt] + h, "turned%d%d" % (nt, h))
+                    turn_half(turned[nt, h], based[nt], h, True, False)
+                else:
+                    summed[nt, h] = bank(6 + h, "summed%d%d" % (nt, h))
+                    turn_half(summed[nt, h], based[nt], h, True, False)
+
+        def turn_page(e, nt):
+            for h in range(2):
+                if nt == 3:
+                    turned[nt, h] = bank(2 + h, "turned%d%d" % (nt, h))
+                turn_half(turned[nt, h], pages[e][nt % 2], h, nt == 3, e == 1 or nt == 3)
+
+        def turn_back(nt):
+            for h in range(2):
+                held = sb("held%d%d" % (nt, h), [P, BANK], F32, tag="held%d%d" % (nt % 2, h))
+                nc.scalar.copy(out=held[:], in_=turned[nt, h][:])
+                if nt < 3:
+                    summed[nt, h] = bank(h, "summed%d%d" % (nt, h))
+                turn_half(summed[nt, h], held, 0, nt < 3, True)
+
+        def store(nt):
+            for h in range(2):
+                done = sb("done%d%d" % (nt, h), [P, BANK], F32)
+                cols = slice(BANK * h, BANK * (h + 1))
+                if nt < 3:
+                    nc.scalar.copy(out=done[:], in_=summed[nt, h][:])
+                else:
+                    nc.vector.tensor_tensor(out=done[:], in0=summed[nt, h][:], in1=pages[1][nt % 2][:, cols], op=ADD)
+                nc.sync.dma_start(out=out[P * nt : P * (nt + 1), cols], in_=done[:])
+
+        gather_plane(0)
+        gather_words(0, 0, 512)
+        deal(low_words[0][:], la_raw[:])
+        deal(low_plane[:], low_plane_raw[:])
+        lb_raw = sb("lb_raw", [P, R], I32, tag="raw_words")
+        nc.sync.dma_start(out=lb_raw[:], in_=fp8_words(lb_words))
+        load_scale_rows(late_planes[:, 0:N], ub_scales, 0)
+        load_scale_rows(ws_plane, ws_scales, 0)
+        for c in range(4):
+            lower(0, c, c)
+        ub_w = sb("ub_w", [P, 2 * N], U8, tag="first_words")
+        up_words.append(ub_w)
+        nc.sync.dma_start(out=ub_w[:].bitcast(I32), in_=ub_words[0].bitcast(I32))
+        g_words.append(shared.tile([P, J], I32, name="g_words1", align_bytes=64, offset=0))
+        g_plane.append(shared.tile([P, J], U8, name="g_plane1", align_bytes=64, offset=4 * J))
+        gather_plane(1)
+        gather_words(1, 0, 512)
+        quantise(0, 0)
+        upper(0, 0, 4, 0, 256)
+        deal(low_words[1][:], lb_raw[:])
+        quantise(0, 1)
+        upper(0, 0, 5, 256, 512)
+        ws_w = sb("ws_w", [P, 2 * N], U8, tag="raw_words")
+        nc.sync.dma_start(out=ws_w[:].bitcast(I32), in_=ws_words[0].bitcast(I32))
+        scatter(0, 0, 0, 256)
+        for c in range(4):
+            lower(1, c, 4 + c % 2)
+        upper(0, 1, 4, 0, 512)
+        scatter(0, 0, 256, 512)
+        quantise(1, 0)
+        upper(1, 0, 6, 0, 256)
+        quantise(1, 1)
+        upper(1, 0, 7, 256, 512)
+        scatter(0, 1, 0, 512)
+        upper(1, 1, 6, 0, 512)
+        upper(0, 2, 7, 0, 512)
+        upper(1, 2, 5, 0, 512)
+        base(0)
+        turn_base(0)
+        turn_page(0, 0)
+        base(1)
+        scatter(1, 0, 0, 512)
+        turn_base(1)
+        turn_page(0, 1)
+        base(2)
+        base(3)
+        turn_page(1, 0)
+        scatter(1, 1, 0, 512)
+        turn_back(0)
+        store(0)
+        upper(0, 3, 0, 0, 512)
+        turn_base(2)
+        turn_page(1, 1)
+        scatter(0, 2, 0, 512)
+        turn_back(1)
+        store(1)
+        upper(1, 3, 0, 0, 512)
+        turn_base(3)
+        turn_page(0, 2)
+        scatter(1, 2, 0, 512)
+        turn_page(1, 2)
+        scatter(0, 3, 0, 512)
+        turn_back(2)
+        store(2)
+        turn_page(0, 3)
+        scatter(1, 3, 0, 512)
+        turn_back(3)
+        store(3)

@@ -39,8 +39,8 @@ def tile_list_two_experts_on_base_kernel(
         def bank(b, name):
             return psum.tile([P, BANK], F32, name=name, tag="bank%d" % b)
 
-        def load_scale_rows(plane, rows, first):
-            for q in range(4):
+        def load_scale_rows(plane, rows, first, quadrants=range(4)):
+            for q in quadrants:
                 nc.sync.dma_start(
                     out=plane[32 * q + first : 32 * q + first + 4, :].bitcast(I32),
                     in_=rows[0, 4 * q : 4 * q + 4, :].bitcast(I32),
@@ -56,41 +56,48 @@ def tile_list_two_experts_on_base_kernel(
         low_plane_raw = shared.tile([P, R], U8, name="low_plane_raw", align_bytes=64, offset=4 * J - 256)
         ua_plane = sb("ua_plane", [P, N], U8)
         late_planes = sb("late_planes", [P, 2 * N], U8)
-        la_raw = sb("la_raw", [P, R], I32, tag="raw_words")
+        la_raw = sb("la_raw", [P, R], I32)
+        lb_raw = sb("lb_raw", [P, R], I32)
         ua_w = sb("ua_w", [P, 2 * N], U8)
+        ub_w = sb("ub_w", [P, 2 * N], U8)
+        ws_w = sb("ws_w", [P, 2 * N], U8)
         pages = [[sb("page%d%d" % (e, s), [P, T], F32) for s in range(2)] for e in range(2)]
         ident = sb("ident", [P, P], F32)
 
-        nc.gpsimd.memset(x_plane[:].bitcast(I32), 0)
-        nc.gpsimd.memset(low_plane_raw[:].bitcast(I32), 0)
-        nc.vector.memset(ua_plane[:].bitcast(I32), 0)
+        for plane in (x_plane, low_plane_raw, ua_plane, late_planes):
+            nc.gpsimd.memset(plane[:].bitcast(I32), 0)
+        make_identity(nc, ident[:])
+        for s in range(2):
+            nc.vector.memset(pages[0][s][:], 0.0)
+            nc.gpsimd.memset(pages[1][s][:], 0.0)
         nc.sync.dma_start(list_a[:], offs)
-        nc.sync.dma_start(list_b[:], offs2)
         load_scale_rows(x_plane, xq_scales, 0)
+        load_scale_rows(low_plane_raw, la_scales, 0, range(0, 2))
         nc.sync.dma_start(out=x_words[:], in_=fp8_words(xq_words))
         nc.sync.dma_start(out=la_raw[:], in_=fp8_words(la_words))
-        load_scale_rows(low_plane_raw, la_scales, 0)
+        load_scale_rows(low_plane_raw, la_scales, 0, range(2, 4))
         load_scale_rows(low_plane_raw, lb_scales, 4)
+        nc.sync.dma_start(list_b[:], offs2)
+        nc.sync.dma_start(out=lb_raw[:], in_=fp8_words(lb_words))
         nc.sync.dma_start(out=ua_w[:].bitcast(I32), in_=ua_words[0].bitcast(I32))
         load_scale_rows(ua_plane, ua_scales, 0)
-        for e in range(2):
-            for s in range(2):
-                nc.vector.memset(pages[e][s][:], 0.0)
-        nc.vector.memset(late_planes[:].bitcast(I32), 0)
-        make_identity(nc, ident[:])
+        load_scale_rows(late_planes[:, 0:N], ub_scales, 0)
+        nc.sync.dma_start(out=ub_w[:].bitcast(I32), in_=ub_words[0].bitcast(I32))
+        load_scale_rows(late_planes[:, N : 2 * N], ws_scales, 0)
+        nc.sync.dma_start(out=ws_w[:].bitcast(I32), in_=ws_words[0].bitcast(I32))
 
         lists = [list_a, list_b]
-        g_words = [sb("g_words0", [P, J], I32, tag="first_words")]
+        g_words = [sb("g_words0", [P, J], I32)]
         g_plane = [sb("g_plane0", [P, J], U8)]
-        low_words = [sb("low_words%d" % e, [P, R], I32) for e in range(2)]
+        low_words = [sb("low_words0", [P, R], I32)]
         low_plane = sb("low_plane", [P, R], U8)
         mid_bf = [[sb("mid_bf%d%d" % (e, h), [P, 2, P, PACK], BF16) for h in range(2)] for e in range(2)]
         mid_words = [sb("mid_words%d" % e, [P, J], I32) for e in range(2)]
         mid_plane = [sb("mid_plane%d" % e, [P, J], U8) for e in range(2)]
-        up_words = [ua_w]
+        up_words = [ua_w, ub_w]
         up_planes = [ua_plane[:], late_planes[:, 0:N]]
         ws_plane = late_planes[:, N : 2 * N]
-        results = [[sb("res%d%d" % (e, nt), [P, J], F32) for nt in range(4)] for e in range(2)]
+        results = {}
 
         def gather_plane(e):
             nc.vector.tensor_copy(out=g_plane[e][:], in_=x_plane[:].indirect(lists[e][:]))
@@ -141,12 +148,15 @@ def tile_list_two_experts_on_base_kernel(
                 start=True,
                 stop=True,
             )
-            nc.scalar.copy(out=results[e][nt][:, lo:hi], in_=acc[:, 0 : hi - lo])
+            if lo == 0:
+                name = "res%d%d" % (e, nt)
+                results[e, nt] = sb(name, [P, J], F32, tag="lb_raw" if (e, nt) == (0, 0) else name)
+            nc.scalar.copy(out=results[e, nt][:, lo:hi], in_=acc[:, 0 : hi - lo])
 
         def scatter(e, nt, lo, hi):
             nc.vector.tensor_copy(
                 out=pages[e][nt % 2][:].indirect(lists[e][:, lo // 16 : hi // 16]),
-                in_=results[e][nt][:, lo:hi],
+                in_=results[e, nt][:, lo:hi],
             )
 
         def turn_add(acc, c, src, start, stop):
@@ -221,47 +231,47 @@ def tile_list_two_experts_on_base_kernel(
                 cols = slice(BANK * h, BANK * (h + 1))
                 if nt < 3:
                     nc.scalar.copy(out=done[:], in_=summed[nt, h][:])
+                    nc.sync.dma_start(out=out[P * nt : P * (nt + 1), cols], in_=done[:])
                 else:
-                    nc.vector.tensor_tensor(out=done[:], in0=summed[nt, h][:], in1=pages[1][nt % 2][:, cols], op=ADD)
-                nc.sync.dma_start(out=out[P * nt : P * (nt + 1), cols], in_=done[:])
+                    step = BANK // (h + 1)
+                    for lo in range(0, BANK, step):
+                        toks = slice(BANK * h + lo, BANK * h + lo + step)
+                        nc.vector.tensor_tensor(
+                            out=done[:, lo : lo + step],
+                            in0=summed[nt, h][:, lo : lo + step],
+                            in1=pages[1][nt % 2][:, toks],
+                            op=ADD,
+                        )
+                        nc.sync.dma_start(out=out[P * nt : P * (nt + 1), toks], in_=done[:, lo : lo + step])
 
         gather_plane(0)
         gather_words(0, 0, 512)
         deal(low_words[0][:], la_raw[:])
         deal(low_plane[:], low_plane_raw[:])
-        lb_raw = sb("lb_raw", [P, R], I32, tag="raw_words")
-        nc.sync.dma_start(out=lb_raw[:], in_=fp8_words(lb_words))
-        load_scale_rows(late_planes[:, 0:N], ub_scales, 0)
-        load_scale_rows(ws_plane, ws_scales, 0)
         for c in range(4):
             lower(0, c, c)
-        ub_w = sb("ub_w", [P, 2 * N], U8, tag="first_words")
-        up_words.append(ub_w)
-        nc.sync.dma_start(out=ub_w[:].bitcast(I32), in_=ub_words[0].bitcast(I32))
         g_words.append(shared.tile([P, J], I32, name="g_words1", align_bytes=64, offset=0))
         g_plane.append(shared.tile([P, J], U8, name="g_plane1", align_bytes=64, offset=4 * J))
         gather_plane(1)
         gather_words(1, 0, 512)
         quantise(0, 0)
-        upper(0, 0, 4, 0, 256)
-        deal(low_words[1][:], lb_raw[:])
         quantise(0, 1)
+        low_words.append(sb("low_words1", [P, R], I32, tag="mid_bf01"))
+        deal(low_words[1][:], lb_raw[:])
+        upper(0, 0, 4, 0, 256)
         upper(0, 0, 5, 256, 512)
-        ws_w = sb("ws_w", [P, 2 * N], U8, tag="raw_words")
-        nc.sync.dma_start(out=ws_w[:].bitcast(I32), in_=ws_words[0].bitcast(I32))
         scatter(0, 0, 0, 256)
         for c in range(4):
-            lower(1, c, 4 + c % 2)
-        upper(0, 1, 4, 0, 512)
+            lower(1, c, c)
+        upper(0, 1, 2, 0, 512)
         scatter(0, 0, 256, 512)
         quantise(1, 0)
-        upper(1, 0, 6, 0, 256)
         quantise(1, 1)
-        upper(1, 0, 7, 256, 512)
+        upper(1, 0, 2, 0, 512)
         scatter(0, 1, 0, 512)
-        upper(1, 1, 6, 0, 512)
-        upper(0, 2, 7, 0, 512)
-        upper(1, 2, 5, 0, 512)
+        upper(1, 1, 2, 0, 512)
+        upper(1, 2, 4, 0, 512)
+        upper(0, 2, 5, 0, 512)
         base(0)
         turn_base(0)
         turn_page(0, 0)

@@ -69,7 +69,7 @@ def tile_list_two_experts_on_base_kernel(
         make_identity(nc, ident[:])
         for s in range(2):
             nc.vector.memset(pages[0][s][:], 0.0)
-            nc.gpsimd.memset(pages[1][s][:], 0.0)
+            nc.vector.memset(pages[1][s][:], 0.0)
         nc.sync.dma_start(list_a[:], offs)
         load_scale_rows(x_plane, xq_scales, 0)
         load_scale_rows(low_plane_raw, la_scales, 0, range(0, 2))
@@ -108,9 +108,10 @@ def tile_list_two_experts_on_base_kernel(
                 in_=x_words[:].bitcast(U32).indirect(lists[e][:, lo // 16 : hi // 16]),
             )
 
-        def deal(dst, src):
+        def deal(dst, src, run):
             nc.vector.tensor_copy(
-                out=dst.rearrange("p (t m) -> p m t", t=PACK), in_=src.rearrange("p (m t) -> p m t", t=PACK)
+                out=dst.rearrange("p (t b m) -> p b t m", t=PACK, m=run),
+                in_=src.rearrange("p (b m t) -> p b t m", t=PACK, m=run),
             )
 
         def lower(e, c, b):
@@ -246,8 +247,8 @@ def tile_list_two_experts_on_base_kernel(
 
         gather_plane(0)
         gather_words(0, 0, 512)
-        deal(low_words[0][:], la_raw[:])
-        deal(low_plane[:], low_plane_raw[:])
+        deal(low_words[0][:], la_raw[:], 4)
+        deal(low_plane[:], low_plane_raw[:], 16)
         for c in range(4):
             lower(0, c, c)
         g_words.append(shared.tile([P, J], I32, name="g_words1", align_bytes=64, offset=0))
@@ -257,7 +258,7 @@ def tile_list_two_experts_on_base_kernel(
         quantise(0, 0)
         quantise(0, 1)
         low_words.append(sb("low_words1", [P, R], I32, tag="mid_bf01"))
-        deal(low_words[1][:], lb_raw[:])
+        deal(low_words[1][:], lb_raw[:], 4)
         upper(0, 0, 4, 0, 256)
         upper(0, 0, 5, 256, 512)
         scatter(0, 0, 0, 256)

@@ -69,7 +69,7 @@ def tile_list_two_experts_on_base_kernel(
         make_identity(nc, ident[:])
         for s in range(2):
             nc.vector.memset(pages[0][s][:], 0.0)
-            nc.vector.memset(pages[1][s][:], 0.0)
+            nc.gpsimd.memset(pages[1][s][:], 0.0)
         nc.sync.dma_start(list_a[:], offs)
         load_scale_rows(x_plane, xq_scales, 0)
         load_scale_rows(low_plane_raw, la_scales, 0, range(0, 2))
@@ -81,10 +81,10 @@ def tile_list_two_experts_on_base_kernel(
         nc.sync.dma_start(out=lb_raw[:], in_=fp8_words(lb_words))
         nc.sync.dma_start(out=ua_w[:].bitcast(I32), in_=ua_words[0].bitcast(I32))
         load_scale_rows(ua_plane, ua_scales, 0)
-        load_scale_rows(late_planes[:, 0:N], ub_scales, 0)
-        nc.sync.dma_start(out=ub_w[:].bitcast(I32), in_=ub_words[0].bitcast(I32))
         load_scale_rows(late_planes[:, N : 2 * N], ws_scales, 0)
         nc.sync.dma_start(out=ws_w[:].bitcast(I32), in_=ws_words[0].bitcast(I32))
+        load_scale_rows(late_planes[:, 0:N], ub_scales, 0)
+        nc.sync.dma_start(out=ub_w[:].bitcast(I32), in_=ub_words[0].bitcast(I32))
 
         lists = [list_a, list_b]
         g_words = [sb("g_words0", [P, J], I32)]
@@ -108,10 +108,9 @@ def tile_list_two_experts_on_base_kernel(
                 in_=x_words[:].bitcast(U32).indirect(lists[e][:, lo // 16 : hi // 16]),
             )
 
-        def deal(dst, src, run):
+        def deal(dst, src):
             nc.vector.tensor_copy(
-                out=dst.rearrange("p (t b m) -> p b t m", t=PACK, m=run),
-                in_=src.rearrange("p (b m t) -> p b t m", t=PACK, m=run),
+                out=dst.rearrange("p (t m) -> p m t", t=PACK), in_=src.rearrange("p (m t) -> p m t", t=PACK)
             )
 
         def lower(e, c, b):
@@ -169,10 +168,10 @@ def tile_list_two_experts_on_base_kernel(
         turned = {}
         summed = {}
 
-        def base(nt):
+        def base(nt, first_bank):
             based[nt] = sb("based%d" % nt, [P, T], F32)
             for h in range(2):
-                acc = bank(4 + h, "base%d%d" % (nt, h))
+                acc = bank(first_bank + h, "base%d%d" % (nt, h))
                 cols = slice(BANK * h, BANK * (h + 1))
                 if nt < 3:
                     nc.tensor.matmul_mx(
@@ -205,18 +204,18 @@ def tile_list_two_experts_on_base_kernel(
 
         def turn_base(nt):
             for h in range(2):
-                if nt < 3:
-                    turned[nt, h] = bank((2, 6, 2)[nt] + h, "turned%d%d" % (nt, h))
-                    turn_half(turned[nt, h], based[nt], h, True, False)
-                else:
+                if nt == 2:
+                    turned[nt, h] = bank(2 + h, "turned%d%d" % (nt, h))
+                if nt == 3:
                     summed[nt, h] = bank(6 + h, "summed%d%d" % (nt, h))
-                    turn_half(summed[nt, h], based[nt], h, True, False)
+                turn_half((summed if nt == 3 else turned)[nt, h], based[nt], h, nt >= 2, False)
 
         def turn_page(e, nt):
+            opens = e == 0 and nt != 2
             for h in range(2):
-                if nt == 3:
-                    turned[nt, h] = bank(2 + h, "turned%d%d" % (nt, h))
-                turn_half(turned[nt, h], pages[e][nt % 2], h, nt == 3, e == 1 or nt == 3)
+                if opens:
+                    turned[nt, h] = bank((6 if nt == 1 else 2) + h, "turned%d%d" % (nt, h))
+                turn_half(turned[nt, h], pages[e][nt % 2], h, opens, e == 1 or nt == 3)
 
         def turn_back(nt):
             for h in range(2):
@@ -247,8 +246,8 @@ def tile_list_two_experts_on_base_kernel(
 
         gather_plane(0)
         gather_words(0, 0, 512)
-        deal(low_words[0][:], la_raw[:], 4)
-        deal(low_plane[:], low_plane_raw[:], 16)
+        deal(low_words[0][:], la_raw[:])
+        deal(low_plane[:], low_plane_raw[:])
         for c in range(4):
             lower(0, c, c)
         g_words.append(shared.tile([P, J], I32, name="g_words1", align_bytes=64, offset=0))
@@ -258,7 +257,7 @@ def tile_list_two_experts_on_base_kernel(
         quantise(0, 0)
         quantise(0, 1)
         low_words.append(sb("low_words1", [P, R], I32, tag="mid_bf01"))
-        deal(low_words[1][:], lb_raw[:], 4)
+        deal(low_words[1][:], lb_raw[:])
         upper(0, 0, 4, 0, 256)
         upper(0, 0, 5, 256, 512)
         scatter(0, 0, 0, 256)
@@ -266,35 +265,36 @@ def tile_list_two_experts_on_base_kernel(
             lower(1, c, c)
         upper(0, 1, 2, 0, 512)
         scatter(0, 0, 256, 512)
+        base(2, 4)
+        base(3, 6)
         quantise(1, 0)
         quantise(1, 1)
-        upper(1, 0, 2, 0, 512)
+        upper(1, 0, 6, 0, 512)
         scatter(0, 1, 0, 512)
-        upper(1, 1, 2, 0, 512)
-        upper(1, 2, 4, 0, 512)
-        upper(0, 2, 5, 0, 512)
-        base(0)
-        turn_base(0)
+        upper(1, 1, 7, 0, 512)
+        upper(0, 2, 7, 0, 512)
+        upper(1, 2, 4, 0, 256)
+        upper(1, 2, 5, 256, 512)
         turn_page(0, 0)
-        base(1)
+        base(0, 4)
         scatter(1, 0, 0, 512)
-        turn_base(1)
+        base(1, 4)
         turn_page(0, 1)
-        base(2)
-        base(3)
+        turn_base(0)
         turn_page(1, 0)
+        turn_base(1)
         scatter(1, 1, 0, 512)
         turn_back(0)
         store(0)
-        upper(0, 3, 0, 0, 512)
-        turn_base(2)
+        upper(0, 3, 2, 0, 512)
+        upper(1, 3, 3, 0, 512)
         turn_page(1, 1)
+        turn_base(2)
         scatter(0, 2, 0, 512)
         turn_back(1)
         store(1)
-        upper(1, 3, 0, 0, 512)
-        turn_base(3)
         turn_page(0, 2)
+        turn_base(3)
         scatter(1, 2, 0, 512)
         turn_page(1, 2)
         scatter(0, 3, 0, 512)

@@ -207,7 +207,7 @@ def tile_list_two_experts_on_base_kernel(
                 if nt == 2:
                     turned[nt, h] = bank(2 + h, "turned%d%d" % (nt, h))
                 if nt == 3:
-                    summed[nt, h] = bank(6 + h, "summed%d%d" % (nt, h))
+                    summed[nt, h] = bank(h, "summed%d%d" % (nt, h))
                 turn_half((summed if nt == 3 else turned)[nt, h], based[nt], h, nt >= 2, False)
 
         def turn_page(e, nt):
@@ -222,7 +222,7 @@ def tile_list_two_experts_on_base_kernel(
                 held = sb("held%d%d" % (nt, h), [P, BANK], F32, tag="held%d%d" % (nt % 2, h))
                 nc.scalar.copy(out=held[:], in_=turned[nt, h][:])
                 if nt < 3:
-                    summed[nt, h] = bank(h, "summed%d%d" % (nt, h))
+                    summed[nt, h] = bank(4 + h, "summed%d%d" % (nt, h))
                 turn_half(summed[nt, h], held, 0, nt < 3, True)
 
         def store(nt):
@@ -276,6 +276,7 @@ def tile_list_two_experts_on_base_kernel(
         upper(1, 2, 4, 0, 256)
         upper(1, 2, 5, 256, 512)
         turn_page(0, 0)
+        turn_base(3)
         base(0, 4)
         scatter(1, 0, 0, 512)
         base(1, 4)
@@ -294,7 +295,6 @@ def tile_list_two_experts_on_base_kernel(
         turn_back(1)
         store(1)
         turn_page(0, 2)
-        turn_base(3)
         scatter(1, 2, 0, 512)
         turn_page(1, 2)
         scatter(0, 3, 0, 512)

from contextlib import ExitStack

import concourse.mybir as mybir
from concourse.masks import make_identity

K, T, J, N, R = 512, 1024, 512, 512, 512
FLOPS = 2 * K * N * T + 2 * (2 * K * R * J + 2 * R * N * J)

F32 = mybir.dt.float32
BF16 = mybir.dt.bfloat16
I32 = mybir.dt.int32
U32 = mybir.dt.uint32
U16 = mybir.dt.uint16
U8 = mybir.dt.uint8
FP8X4 = mybir.dt.float8_e4m3fn_x4
FP4X4 = mybir.dt.float4_e2m1fn_x4
COPY = mybir.ActivationFunctionType.Copy
ADD = mybir.AluOpType.add

P = 128
PACK = 4
BANK = 512
BASE_GAIN = 0.4


def tile_list_two_experts_on_base_kernel(
    tc, xq_words, xq_scales, ws_words, ws_scales, la_words, la_scales, ua_words, ua_scales,
    lb_words, lb_scales, ub_words, ub_scales, offs, offs2, out,
):
    nc = tc.nc
    with ExitStack() as ctx:
        keep = ctx.enter_context(tc.tile_pool(name="keep", bufs=1))
        shared = ctx.enter_context(tc.tile_pool(name="shared", bufs=1))
        psum = ctx.enter_context(tc.psum_pool(name="psum", bufs=1))

        def sb(name, shape, dtype, tag=None):
            return keep.tile(shape, dtype, name=name, tag=tag or name, align_bytes=64)

        def bank(b, name):
            return psum.tile([P, BANK], F32, name=name, tag="bank%d" % b)

        def load_scale_rows(plane, rows, first, quadrants=range(4)):
            for q in quadrants:
                nc.sync.dma_start(
                    out=plane[32 * q + first : 32 * q + first + 4, :].bitcast(I32),
                    in_=rows[0, 4 * q : 4 * q + 4, :].bitcast(I32),
                )

        def fp8_words(words):
            return words[0].rearrange("p n t -> p (n t)").bitcast(I32)

        list_a = keep.tile([P, J // 16], U16, name="list_a")
        list_b = keep.tile([P, J // 16], U16, name="list_b")
        x_words = sb("x_words", [P, T], I32)
        x_plane = sb("x_plane", [P, T], U8)
        low_plane_raw = shared.tile([P, R], U8, name="low_plane_raw", align_bytes=64, offset=4 * J - 256)
        ua_plane = sb("ua_plane", [P, N], U8)
        late_planes = sb("late_planes", [P, 2 * N], U8)
        la_raw = sb("la_raw", [P, R], I32)
        lb_raw = sb("lb_raw", [P, R], I32)
        ua_w = sb("ua_w", [P, 2 * N], U8)
        ub_w = sb("ub_w", [P, 2 * N], U8)
        ws_w = sb("ws_w", [P, 2 * N], U8)
        pages = [[sb("page%d%d" % (e, s), [P, T], F32) for s in range(2)] for e in range(2)]
        ident = sb("ident", [P, P], F32)

        for plane in (x_plane, low_plane_raw, ua_plane, late_planes):
            nc.gpsimd.memset(plane[:].bitcast(I32), 0)
        make_identity(nc, ident[:])
        for s in range(2):
            nc.vector.memset(pages[0][s][:], 0.0)
            nc.gpsimd.memset(pages[1][s][:], 0.0)
        nc.sync.dma_start(list_a[:], offs)
        load_scale_rows(x_plane, xq_scales, 0)
        load_scale_rows(low_plane_raw, la_scales, 0, range(0, 2))
        nc.sync.dma_start(out=x_words[:], in_=fp8_words(xq_words))
        nc.sync.dma_start(out=la_raw[:], in_=fp8_words(la_words))
        load_scale_rows(low_plane_raw, la_scales, 0, range(2, 4))
        load_scale_rows(low_plane_raw, lb_scales, 4)
        nc.sync.dma_start(list_b[:], offs2)
        nc.sync.dma_start(out=lb_raw[:], in_=fp8_words(lb_words))
        nc.sync.dma_start(out=ua_w[:].bitcast(I32), in_=ua_words[0].bitcast(I32))
        load_scale_rows(ua_plane, ua_scales, 0)
        load_scale_rows(late_planes[:, N : 2 * N], ws_scales, 0)
        nc.sync.dma_start(out=ws_w[:].bitcast(I32), in_=ws_words[0].bitcast(I32))
        load_scale_rows(late_planes[:, 0:N], ub_scales, 0)
        nc.sync.dma_start(out=ub_w[:].bitcast(I32), in_=ub_words[0].bitcast(I32))

        lists = [list_a, list_b]
        g_words = [sb("g_words0", [P, J], I32)]
        g_plane = [sb("g_plane0", [P, J], U8)]
        low_words = [sb("low_words0", [P, R], I32)]
        low_plane = sb("low_plane", [P, R], U8)
        mid_bf = [[sb("mid_bf%d%d" % (e, h), [P, 2, P, PACK], BF16) for h in range(2)] for e in range(2)]
        mid_words = [sb("mid_words%d" % e, [P, J], I32) for e in range(2)]
        mid_plane = [sb("mid_plane%d" % e, [P, J], U8) for e in range(2)]
        up_words = [ua_w, ub_w]
        up_planes = [ua_plane[:], late_planes[:, 0:N]]
        ws_plane = late_planes[:, N : 2 * N]
        results = {}

        def gather_plane(e):
            nc.vector.tensor_copy(out=g_plane[e][:], in_=x_plane[:].indirect(lists[e][:]))

        def gather_words(e, lo, hi):
            nc.vector.tensor_copy(
                out=g_words[e][:, lo:hi].bitcast(U32),
                in_=x_words[:].bitcast(U32).indirect(lists[e][:, lo // 16 : hi // 16]),
            )

        def deal(dst, src):
            nc.vector.tensor_copy(
                out=dst.rearrange("p (t m) -> p m t", t=PACK), in_=src.rearrange("p (m t) -> p m t", t=PACK)
            )

        def lower(e, c, b):
            acc = bank(b, "low%d%d" % (e, c))
            cols = slice(P * c, P * (c + 1))
            for t in range(PACK):
                tc_ = slice(P * t, P * (t + 1))
                nc.tensor.matmul_mx(
                    out=acc[:, tc_],
                    lhsT=low_words[e][:, tc_].bitcast(FP8X4),
                    lhsT_scale=low_plane[4 * e : P, tc_],
                    rhs=g_words[e][:, cols].bitcast(FP8X4),
                    rhs_scale=g_plane[e][:, cols],
                    start=True,
                    stop=True,
                )
            nc.scalar.copy(out=mid_bf[e][c // 2][:, c % 2, :, :], in_=acc[:].rearrange("p (t j) -> p j t", t=PACK))

        def quantise(e, h):
            cols = slice(256 * h, 256 * (h + 1))
            nc.vector.quantize_mx(
                out=mid_words[e][:, cols].bitcast(FP8X4),
                scales=mid_plane[e][:, cols],
                in_=mid_bf[e][h][:].rearrange("p c j t -> p (c j t)"),
            )

        def upper(e, nt, b, lo, hi):
            acc = bank(b, "up%d%d_%d" % (e, nt, lo))
            nc.tensor.matmul_mx(
                out=acc[:, 0 : hi - lo],
                lhsT=up_words[e][:, 2 * P * nt : 2 * P * (nt + 1)].bitcast(FP4X4),
                lhsT_scale=up_planes[e][:, P * nt : P * (nt + 1)],
                rhs=mid_words[e][:, lo:hi].bitcast(FP8X4),
                rhs_scale=mid_plane[e][:, lo:hi],
                start=True,
                stop=True,
            )
            if lo == 0:
                name = "res%d%d" % (e, nt)
                results[e, nt] = sb(name, [P, J], F32, tag="lb_raw" if (e, nt) == (0, 0) else name)
            nc.scalar.copy(out=results[e, nt][:, lo:hi], in_=acc[:, 0 : hi - lo])

        def scatter(e, nt, lo, hi):
            nc.vector.tensor_copy(
                out=pages[e][nt % 2][:].indirect(lists[e][:, lo // 16 : hi // 16]),
                in_=results[e, nt][:, lo:hi],
            )

        def turn_add(acc, c, src, start, stop):
            nc.tensor.matmul(
                out=acc[:, P * c : P * (c + 1)], lhsT=src, rhs=ident[:], start=start, stop=stop, is_transpose=True
            )

        based = {}
        turned = {}
        summed = {}

        def base(nt, first_bank):
            based[nt] = sb("based%d" % nt, [P, T], F32)
            for h in range(2):
                acc = bank(first_bank + h, "base%d%d" % (nt, h))
                cols = slice(BANK * h, BANK * (h + 1))
                if nt < 3:
                    nc.tensor.matmul_mx(
                        out=acc[:],
                        lhsT=ws_w[:, 2 * P * nt : 2 * P * (nt + 1)].bitcast(FP4X4),
                        lhsT_scale=ws_plane[:, P * nt : P * (nt + 1)],
                        rhs=x_words[:, cols].bitcast(FP8X4),
                        rhs_scale=x_plane[:, cols],
                        start=True,
                        stop=True,
                    )
                else:
                    for c in range(4):
                        toks = slice(BANK * h + P * c, BANK * h + P * (c + 1))
                        nc.tensor.matmul_mx(
                            out=acc[:, P * c : P * (c + 1)],
                            lhsT=x_words[:, toks].bitcast(FP8X4),
                            lhsT_scale=x_plane[:, toks],
                            rhs=ws_w[:, 2 * P * nt : 2 * P * (nt + 1)].bitcast(FP4X4),
                            rhs_scale=ws_plane[:, P * nt : P * (nt + 1)],
                            start=True,
                            stop=True,
                        )
                nc.scalar.activation(out=based[nt][:, cols], in_=acc[:], func=COPY, scale=BASE_GAIN)

        def turn_half(acc, src, h, start, stop):
            for c in range(4):
                tb = 4 * h + c
                turn_add(acc, c, src[:, P * tb : P * (tb + 1)], start and c == 0, stop and c == 3)

        def turn_base(nt):
            for h in range(2):
                if nt == 2:
                    turned[nt, h] = bank(2 + h, "turned%d%d" % (nt, h))
                if nt == 3:
                    summed[nt, h] = bank(h, "summed%d%d" % (nt, h))
                turn_half((summed if nt == 3 else turned)[nt, h], based[nt], h, nt >= 2, False)

        def turn_page(e, nt):
            opens = e == 0 and nt != 2
            for h in range(2):
                if opens:
                    turned[nt, h] = bank((6 if nt == 1 else 2) + h, "turned%d%d" % (nt, h))
                turn_half(turned[nt, h], pages[e][nt % 2], h, opens, e == 1 or nt == 3)

        def turn_back(nt):
            for h in range(2):
                held = sb("held%d%d" % (nt, h), [P, BANK], F32, tag="held%d%d" % (nt % 2, h))
                nc.scalar.copy(out=held[:], in_=turned[nt, h][:])
                if nt < 3:
                    summed[nt, h] = bank(4 + h, "summed%d%d" % (nt, h))
                turn_half(summed[nt, h], held, 0, nt < 3, True)

        def store(nt):
            for h in range(2):
                done = sb("done%d%d" % (nt, h), [P, BANK], F32)
                cols = slice(BANK * h, BANK * (h + 1))
                if nt < 3:
                    nc.scalar.copy(out=done[:], in_=summed[nt, h][:])
                    nc.sync.dma_start(out=out[P * nt : P * (nt + 1), cols], in_=done[:])
                else:
                    step = BANK // (h + 1)
                    for lo in range(0, BANK, step):
                        toks = slice(BANK * h + lo, BANK * h + lo + step)
                        nc.vector.tensor_tensor(
                            out=done[:, lo : lo + step],
                            in0=summed[nt, h][:, lo : lo + step],
                            in1=pages[1][nt % 2][:, toks],
                            op=ADD,
                        )
                        nc.sync.dma_start(out=out[P * nt : P * (nt + 1), toks], in_=done[:, lo : lo + step])

        gather_plane(0)
        gather_words(0, 0, 512)
        deal(low_words[0][:], la_raw[:])
        deal(low_plane[:], low_plane_raw[:])
        for c in range(4):
            lower(0, c, c)
        g_words.append(shared.tile([P, J], I32, name="g_words1", align_bytes=64, offset=0))
        g_plane.append(shared.tile([P, J], U8, name="g_plane1", align_bytes=64, offset=4 * J))
        gather_plane(1)
        gather_words(1, 0, 512)
        quantise(0, 0)
        quantise(0, 1)
        low_words.append(sb("low_words1", [P, R], I32, tag="mid_bf01"))
        deal(low_words[1][:], lb_raw[:])
        upper(0, 0, 4, 0, 256)
        upper(0, 0, 5, 256, 512)
        scatter(0, 0, 0, 256)
        for c in range(4):
            lower(1, c, c)
        upper(0, 1, 2, 0, 512)
        scatter(0, 0, 256, 512)
        base(2, 4)
        base(3, 6)
        quantise(1, 0)
        quantise(1, 1)
        upper(1, 0, 6, 0, 512)
        scatter(0, 1, 0, 512)
        upper(1, 1, 7, 0, 512)
        upper(0, 2, 7, 0, 512)
        upper(1, 2, 4, 0, 256)
        upper(1, 2, 5, 256, 512)
        turn_page(0, 0)
        turn_base(3)
        base(0, 4)
        scatter(1, 0, 0, 512)
        base(1, 4)
        turn_page(0, 1)
        turn_base(0)
        turn_page(1, 0)
        turn_base(1)
        scatter(1, 1, 0, 512)
        turn_back(0)
        store(0)
        upper(0, 3, 2, 0, 512)
        upper(1, 3, 3, 0, 512)
        turn_page(1, 1)
        turn_base(2)
        scatter(0, 2, 0, 512)
        turn_back(1)
        store(1)
        turn_page(0, 2)
        scatter(1, 2, 0, 512)
        turn_page(1, 2)
        scatter(0, 3, 0, 512)
        turn_back(2)
        store(2)
        turn_page(0, 3)
        scatter(1, 3, 0, 512)
        turn_back(3)
        store(3)
